import numpy as np
import ml_dtypes


def mxq(x, axis, fmt="e4m3"):
    dtype, down = {"e4m3": (ml_dtypes.float8_e4m3fn, 7), "e5m2": (ml_dtypes.float8_e5m2, 14)}[fmt]
    v = np.moveaxis(np.asarray(x, np.float32).astype(ml_dtypes.bfloat16).astype(np.float64), axis, -1)
    blocks = v.reshape(v.shape[:-1] + (-1, 32))
    amax = np.abs(blocks).max(-1, keepdims=True)
    byte = np.maximum(np.where(amax > 0, np.frexp(amax)[1] - 1 + 127, 0) - down, 1)
    scale = np.exp2(byte - 127.0)
    codes = (blocks / scale).astype(np.float32).astype(dtype).astype(np.float64)
    return np.moveaxis((codes * scale).reshape(v.shape), -1, axis)


WIDE = False


def mx_kscale(k):
    if not WIDE:
        return np.ones(k)
    levels = np.array([10, -10, 5, -5, 0])
    if k % 512:
        return np.exp2(np.random.permutation(np.resize(levels, k // 32))).repeat(32)
    a = np.empty((k // 512, 16))
    for p in range(k // 512):
        a[p, :8] = np.random.permutation(np.resize(levels, 8))
        for g in range(8):
            far = levels[np.abs(levels - a[p, g]) >= 10]
            a[p, g + 8] = far[np.random.randint(len(far))]
    return np.exp2(a.ravel()).repeat(32)


def f64(x):
    return np.asarray(x).astype(np.float64)


def striped(idx):
    return np.tile(idx.reshape(-1, 16).T, (8, 1)).astype(np.uint16)


def unstriped(offs):
    return offs[:16].T.reshape(-1).astype(np.int64)


def striped8(idx):
    return np.concatenate([x.reshape(-1, 16).T for x in idx]).astype(np.uint16)


def runs(offs, k):
    lists = np.stack([offs[16 * r : 16 * r + 16].T.reshape(-1) for r in range(8)]).astype(np.int64)
    return lists[np.arange(k) % 512 // 64]


def pack_weight(w):
    k, n = w.shape
    w = f64(np.asarray(w, np.float32).astype(ml_dtypes.bfloat16)).reshape(k // 32, 32, n)
    amax = np.abs(w).max(1)
    byte = np.clip(np.where(amax > 0, np.frexp(amax)[1] - 1 + 127 - 7, 1), 1, 254)
    scaled = (w * np.exp2(127.0 - byte)[:, None, :]).reshape(k, n).astype(np.float32)
    words = np.ascontiguousarray(scaled.reshape(k // 512, 128, 4, n).transpose(0, 1, 3, 2)).astype(ml_dtypes.float8_e4m3fn).view(np.uint8)
    return words, np.ascontiguousarray(byte.astype(np.uint8).reshape(k // 512, 16, n))


def unpack_weight(words, scales):
    g, p, n, _ = words.shape
    vals = np.ascontiguousarray(words).view(ml_dtypes.float8_e4m3fn).astype(np.float64) * np.repeat(np.exp2(scales.astype(np.float64) - 127.0), 8, axis=1)[..., None]
    return vals.transpose(0, 1, 3, 2).reshape(g * 512, n)


def relu(v):
    return np.maximum(v, 0.0)


K, T, S, N, H = 512, 2048, 512, 512, 512


def setup_inputs():
    n = np.random.standard_normal
    s = mx_kscale(K)[:, None]
    u = mx_kscale(H)
    packed_xT = pack_weight(n((K, T)) * s)
    return {
        "x_words": packed_xT[0],
        "x_scales": packed_xT[1],
        "w1": (n((K, H)) / np.sqrt(K) / s).astype(np.float32),
        "gn": (np.random.uniform(0.5, 1.5, (H, 1)) * u[:, None]).astype(np.float32),
        "w2": (n((H, N)) / np.sqrt(H) / u[:, None]).astype(np.float32),
        "gm": (np.random.uniform(0.5, 1.5, (H, 1)) * u[:, None]).astype(np.float32),
        "w3": (n((H, N)) / np.sqrt(H) / u[:, None]).astype(np.float32),
        "offs": striped(np.random.permutation(T)[:S]),
        "n1": striped8(np.stack([np.random.permutation(S) for _ in range(8)])),
        "n2": striped8(np.stack([np.random.permutation(S) for _ in range(8)])),
        "n3": striped8(np.stack([np.random.permutation(S) for _ in range(8)])),
        "n4": striped8(np.stack([np.random.permutation(S) for _ in range(8)])),
        "n5": striped8(np.stack([np.random.permutation(S) for _ in range(8)])),
    }


def reference(x_words, x_scales, w1, gn, w2, gm, w3, offs, n1, n2, n3, n4, n5):
    xq = unpack_weight(x_words, x_scales)[:, unstriped(offs)]
    y = mxq(f64(w1), 0, "e4m3").T @ xq
    rl = relu(y)
    ds = np.zeros((H, S))
    ds[np.arange(H)[:, None], runs(n1, H)] = rl
    z = f64(gn) * (ds - (0.5 * y))
    a = mxq(f64(w2), 0, "e4m3").T @ mxq(z, 0, "e4m3")
    z2 = f64(gm) * (y[np.arange(H)[:, None], runs(n2, H)] - (y[np.arange(H)[:, None], runs(n3, H)]))
    b = mxq(f64(w3), 0, "e4m3").T @ mxq(z2, 0, "e4m3")
    return 0.75 * (a * (b[np.arange(N)[:, None], runs(n5, N)]) - ((a[np.arange(N)[:, None], runs(n4, N)]) * b))

@@ -1,0 +1,229 @@
+from contextlib import ExitStack
+
+import concourse.mybir as mybir
+from concourse.masks import make_identity
+
+F32 = mybir.dt.float32
+BF16 = mybir.dt.bfloat16
+I32 = mybir.dt.int32
+U32 = mybir.dt.uint32
+U16 = mybir.dt.uint16
+U8 = mybir.dt.uint8
+FP8X4 = mybir.dt.float8_e4m3fn_x4
+ALU = mybir.AluOpType
+ACT = mybir.ActivationFunctionType
+
+P = 128
+PACK = 4
+T = 2048
+S = 512
+HALF = S // 2
+FLOPS = 3 * 2 * 512 * 512 * 512
+
+
+def tile_picked_forkcrossbsendgap_none_p_kernel(tc, x_words, x_scales, w1, gn, w2, gm, w3, offs, n1, n2, n3, n4, n5, out):
+    nc = tc.nc
+    with ExitStack() as ctx:
+        sb = ctx.enter_context(tc.tile_pool(name="sb", bufs=1))
+        ps = ctx.enter_context(tc.psum_pool(name="ps", bufs=1))
+
+        def tiles(name, shape, dtype, count=PACK):
+            return [sb.tile(shape, dtype, name="%s%d" % (name, i), align_bytes=64) for i in range(count)]
+
+        lists = tiles("list", [P, S // 16], U16, 6)
+        l_offs, l1, l2, l3, l4, l5 = lists
+        xw = sb.tile([P, T], I32, name="xw", align_bytes=64)
+        xs = sb.tile([P, T], U8, name="xs", align_bytes=64)
+        gn_sb = sb.tile([P, PACK], F32, name="gn_sb", align_bytes=64)
+        gm_sb = sb.tile([P, PACK], F32, name="gm_sb", align_bytes=64)
+        gh_sb = sb.tile([P, PACK], F32, name="gh_sb", align_bytes=64)
+        w_raw = tiles("w_raw", [P, PACK, S], F32, 3)
+        w_bf = tiles("w_bf", [P, PACK * S], BF16, 3)
+        w_q = tiles("w_q", [P, S], U32, 3)
+        w_s = tiles("w_s", [P, S], U8, 3)
+        xg = sb.tile([P, S], U32, name="xg", align_bytes=64)
+        xsg = sb.tile([P, S], U8, name="xsg", align_bytes=64)
+        ywin = tiles("ywin", [P, 2 * S], F32)
+        dswin = tiles("dswin", [P, 2 * S], F32)
+        bwin = tiles("bwin", [P, 2 * S], F32)
+        awin = tiles("awin", [P, S], F32)
+        apos = tiles("apos", [P, S], F32)
+        ym = tiles("ym", [P, S], F32)
+        ident = sb.tile([P, P], F32, name="ident", align_bytes=64)
+        z_t = tiles("z_t", [P, 2 * S], BF16, 2)
+        zbuf = sb.tile([P, 3 * S], F32, name="zbuf", align_bytes=64)
+        z_words = zbuf[:, S:]
+        z_q = sb.tile([P, S], U32, name="z_q", align_bytes=64)
+        z_s = sb.tile([P, S], U8, name="z_s", align_bytes=64)
+        g3_first = tiles("g3", [P, HALF], F32)
+        g3 = [[g[:] for g in g3_first], [zbuf[:, 2 * S : 2 * S + HALF], zbuf[:, 2 * S + HALF :], g3_first[2][:], g3_first[3][:]]]
+        z2buf = sb.tile([P, 2 * S], F32, name="z2buf", align_bytes=64)
+        z2_f = [zbuf[:, : 2 * S], z2buf[:]]
+        pt = tiles("pt", [P, S], F32)
+        qt = tiles("qt", [P, S], F32)
+        z2_b = [z2buf[:, :S].bitcast(BF16), qt[2][:].bitcast(BF16)]
+        z2_q = tiles("z2_q", [P, HALF], U32, 2)
+        z2_s = tiles("z2_s", [P, HALF], U8, 2)
+        st = tiles("st", [P, S], F32, 3)
+        ot = tiles("ot", [P, S], F32)
+        banks = [ps.tile([P, S], F32, name="bank%d" % i) for i in range(8)]
+
+        def load_w(i, w):
+            nc.sync.dma_start(w_raw[i][:], w.rearrange("(p j) c -> p j c", j=PACK))
+
+        nc.vector.memset(xs[:].bitcast(I32), 0)
+        nc.sync.dma_start(gn_sb[:], gn.rearrange("(p t) o -> p (t o)", t=PACK))
+        load_w(0, w1)
+        for q in range(4):
+            nc.sync.dma_start(xs[32 * q : 32 * q + 4, :].bitcast(I32), x_scales[0, 4 * q : 4 * q + 4, :].bitcast(I32))
+        nc.sync.dma_start(l_offs[:], offs)
+        nc.sync.dma_start(xw[:], x_words[0].rearrange("p n t -> p (n t)").bitcast(I32))
+        nc.sync.dma_start(l1[:], n1)
+        load_w(1, w2)
+        nc.sync.dma_start(gm_sb[:], gm.rearrange("(p t) o -> p (t o)", t=PACK))
+        nc.sync.dma_start(l2[:], n2)
+        nc.sync.dma_start(l3[:], n3)
+        load_w(2, w3)
+        nc.sync.dma_start(l4[:], n4)
+        nc.sync.dma_start(l5[:], n5)
+
+        def deal_views(i, m0, m1):
+            dst = w_bf[i][:].rearrange("p (t m j) -> p m j t", t=PACK, j=PACK)
+            src = w_raw[i][:].rearrange("p j (m t) -> p m j t", t=PACK)
+            return dst[:, m0:m1], src[:, m0:m1]
+
+        def quantize(codes, scales, src):
+            nc.vector.quantize_mx(out=codes[:].bitcast(FP8X4), scales=scales[:], in_=src)
+
+        def product(dst, i, t, codes, scales):
+            cols = slice(P * t, P * (t + 1))
+            nc.tensor.matmul_mx(out=dst, lhsT=w_q[i][:, cols].bitcast(FP8X4), lhsT_scale=w_s[i][:, cols],
+                                rhs=codes.bitcast(FP8X4), rhs_scale=scales, start=True, stop=True)
+
+        def part(lst, c):
+            return lst[:, c * HALF // 16 : (c + 1) * HALF // 16]
+
+        def half(c):
+            return slice(c * HALF, (c + 1) * HALF)
+
+        def block(c):
+            return slice(c * P, (c + 1) * P)
+
+        def turn_add(dst, first, second):
+            nc.tensor.matmul(dst, first, ident[:], start=True, stop=False, is_transpose=True)
+            nc.tensor.matmul(dst, second, ident[:], start=False, stop=True, is_transpose=True)
+
+        make_identity(nc, ident[:])
+        for t in range(PACK):
+            nc.vector.tensor_copy(bwin[t][:, S:], gn_sb[:, t : t + 1].to_broadcast([P, S]))
+        nc.vector.tensor_scalar(gh_sb[:], gn_sb[:], -0.5, None, ALU.mult)
+
+        nc.vector.tensor_copy(*deal_views(0, 0, 88))
+        nc.scalar.copy(*deal_views(0, 88, P))
+        nc.vector.tensor_copy(xsg[:], xs[:].indirect(l_offs[:]))
+        quantize(w_q[0], w_s[0], w_bf[0][:])
+        for c in range(2):
+            nc.vector.tensor_copy(xg[:, half(c)], xw[:].bitcast(U32).indirect(part(l_offs, c)))
+
+        y_parts = [(0, half(0), banks[4][:, half(0)]), (0, half(1), banks[0][:, half(1)])]
+        y_parts.extend((t, slice(0, S), banks[t][:]) for t in range(1, PACK))
+        for t, cols, acc in y_parts:
+            product(acc, 0, t, xg[:, cols], xsg[:, cols])
+        for t, cols, acc in y_parts:
+            nc.scalar.activation(ywin[t][:, S:][:, cols], acc, ACT.Relu)
+        for t, cols, acc in y_parts:
+            nc.scalar.activation(ym[t][:, cols], acc, ACT.Copy, scale=gh_sb[:, t : t + 1])
+        for t, cols, acc in y_parts:
+            nc.scalar.activation(ywin[t][:, cols], acc, ACT.Copy, scale=gm_sb[:, t : t + 1])
+        nc.scalar.copy(*deal_views(1, 0, P))
+        nc.scalar.copy(*deal_views(2, 0, P))
+
+        for c in range(2):
+            nc.vector.tensor_tensor(dswin[0][:].indirect(part(l1, c)), ywin[0][:, S:][:, half(c)], bwin[0][:, S:][:, half(c)], ALU.mult)
+        for t in range(1, PACK):
+            nc.vector.tensor_tensor(dswin[t][:].indirect(l1[:]), ywin[t][:, S:], bwin[t][:, S:], ALU.mult)
+
+        turned = [(banks[5], banks[6]), (banks[7], banks[4])]
+        back = (banks[0], banks[1])
+        for u in range(2):
+            for e in range(2):
+                t = 2 * u + e
+                for c in range(PACK):
+                    at = (c % 2) * HALF + e * P
+                    turn_add(turned[u][c // 2][:, at : at + P], ym[t][:, block(c)], dswin[t][:, block(c)])
+            for h in range(2):
+                nc.scalar.copy(z_t[u][:, h * S : (h + 1) * S].rearrange("j (c p e) -> j c p e", c=2, e=2),
+                               turned[u][h][:].rearrange("j (c e p) -> j c p e", c=2, e=2))
+                for c in range(2 * h, 2 * h + 2):
+                    at = u * HALF + (c % 2) * P
+                    nc.tensor.transpose(back[h][:, at : at + P], z_t[u][:].bitcast(F32)[:, block(c)], ident[:])
+        for h in range(2):
+            nc.scalar.copy(z_words[:, h * S : (h + 1) * S].rearrange("p (j u) -> p j u", u=2),
+                           back[h][:].rearrange("p (u j) -> p j u", u=2))
+
+        def z2_fetch(c):
+            for t in range(PACK):
+                nc.vector.tensor_copy(g3[c][t], ywin[t][:].indirect(part(l3, c)))
+
+        def z2_subtract(c, ts):
+            for t in ts:
+                nc.vector.tensor_tensor(z2_f[c][:, t * HALF : (t + 1) * HALF], ywin[t][:].indirect(part(l2, c)), g3[c][t], ALU.subtract)
+
+        def z2_interleave(c):
+            nc.scalar.copy(z2_b[c].rearrange("p (c i t) -> p c t i", i=4, t=PACK), z2_f[c].rearrange("p (t c i) -> p c t i", t=PACK, i=4))
+
+        a_banks = (banks[2], banks[3], banks[5], banks[6])
+        b_banks = (banks[7], banks[4], banks[0], banks[1])
+
+        def b_products(c):
+            quantize(z2_q[c], z2_s[c], z2_b[c])
+            for t in range(PACK):
+                product(b_banks[t][:, half(c)], 2, t, z2_q[c][:], z2_s[c][:])
+                nc.scalar.copy(bwin[t][:, half(c)], b_banks[t][:, half(c)])
+
+        def q_gather(t, c):
+            nc.vector.tensor_tensor(qt[t][:, half(c)], awin[t][:].indirect(part(l4, c)), bwin[t][:, half(c)], ALU.mult)
+
+        z2_fetch(0)
+        z2_subtract(0, range(2))
+        quantize(w_q[1], w_s[1], w_bf[1][:])
+        quantize(w_q[2], w_s[2], w_bf[2][:])
+        quantize(z_q, z_s, z_words.bitcast(BF16))
+        z2_subtract(0, range(2, PACK))
+        for t in range(PACK):
+            product(a_banks[t][:], 1, t, z_q[:], z_s[:])
+        for t in range(PACK):
+            nc.scalar.activation(awin[t][:], a_banks[t][:], ACT.Copy, scale=-0.75)
+            if t == 0:
+                z2_interleave(0)
+        for t in range(2):
+            nc.scalar.activation(apos[t][:], a_banks[t][:], ACT.Copy, scale=0.75)
+        z2_fetch(1)
+        b_products(0)
+        z2_subtract(1, range(PACK))
+        for t in range(2):
+            q_gather(t, 0)
+        z2_interleave(1)
+        b_products(1)
+        for t in range(2, PACK):
+            nc.scalar.activation(apos[t][:], a_banks[t][:], ACT.Copy, scale=0.75)
+        for t in range(2, PACK):
+            q_gather(t, 0)
+        out_rows = out.rearrange("(p t) n -> p t n", t=PACK)
+        for t in range(PACK - 1):
+            q_gather(t, 1)
+            nc.vector.tensor_tensor(pt[t][:], bwin[t][:].indirect(l5[:]), apos[t][:], ALU.mult)
+            there, again = a_banks[2 * (t % 2)], a_banks[2 * (t % 2) + 1]
+            for c in range(PACK):
+                turn_add(there[:, block(c)], qt[t][:, block(c)], pt[t][:, block(c)])
+            nc.scalar.copy(st[t][:], there[:])
+            for c in range(PACK):
+                nc.tensor.transpose(again[:, block(c)], st[t][:, block(c)], ident[:])
+            nc.scalar.copy(ot[t][:], again[:])
+            nc.sync.dma_start(out_rows[:, t, :], ot[t][:])
+        q_gather(3, 1)
+        for c in range(2):
+            nc.vector.tensor_tensor(pt[3][:, half(c)], bwin[3][:].indirect(part(l5, c)), apos[3][:, half(c)], ALU.mult)
+        for c in range(2):
+            nc.vector.tensor_tensor(ot[3][:, half(c)], pt[3][:, half(c)], qt[3][:, half(c)], ALU.add)
+            nc.sync.dma_start(out_rows[:, 3, half(c)], ot[3][:, half(c)])

@@ -32,7 +32,7 @@ def tile_picked_forkcrossbsendgap_none_p_kernel(tc, x_words, x_scales, w1, gn, w
 
         lists = tiles("list", [P, S // 16], U16, 6)
         l_offs, l1, l2, l3, l4, l5 = lists
-        xw = sb.tile([P, T], I32, name="xw", align_bytes=64)
+        xw = sb.tile([P, T], I32, name="xw", tag="xw", align_bytes=64)
         xs = sb.tile([P, T], U8, name="xs", align_bytes=64)
         gn_sb = sb.tile([P, PACK], F32, name="gn_sb", align_bytes=64)
         gm_sb = sb.tile([P, PACK], F32, name="gm_sb", align_bytes=64)
@@ -42,7 +42,7 @@ def tile_picked_forkcrossbsendgap_none_p_kernel(tc, x_words, x_scales, w1, gn, w
         w_q = tiles("w_q", [P, S], U32, 3)
         w_s = tiles("w_s", [P, S], U8, 3)
         xg = sb.tile([P, S], U32, name="xg", align_bytes=64)
-        xsg = sb.tile([P, S], U8, name="xsg", align_bytes=64)
+        xsg_first = sb.tile([P, HALF], U8, name="xsg_first", align_bytes=64)
         ywin = tiles("ywin", [P, 2 * S], F32)
         dswin = tiles("dswin", [P, 2 * S], F32)
         bwin = tiles("bwin", [P, 2 * S], F32)
@@ -64,7 +64,7 @@ def tile_picked_forkcrossbsendgap_none_p_kernel(tc, x_words, x_scales, w1, gn, w
         z2_b = [z2buf[:, :S].bitcast(BF16), qt[2][:].bitcast(BF16)]
         z2_q = tiles("z2_q", [P, HALF], U32, 2)
         z2_s = tiles("z2_s", [P, HALF], U8, 2)
-        st = tiles("st", [P, S], F32, 3)
+        st = tiles("st", [P, S], F32)
         ot = tiles("ot", [P, S], F32)
         banks = [ps.tile([P, S], F32, name="bank%d" % i) for i in range(8)]
 
@@ -109,9 +109,8 @@ def tile_picked_forkcrossbsendgap_none_p_kernel(tc, x_words, x_scales, w1, gn, w
         def block(c):
             return slice(c * P, (c + 1) * P)
 
-        def turn_add(dst, first, second):
-            nc.tensor.matmul(dst, first, ident[:], start=True, stop=False, is_transpose=True)
-            nc.tensor.matmul(dst, second, ident[:], start=False, stop=True, is_transpose=True)
+        def turn(dst, src, start, stop):
+            nc.tensor.matmul(dst, src, ident[:], start=start, stop=stop, is_transpose=True)
 
         make_identity(nc, ident[:])
         for t in range(PACK):
@@ -120,15 +119,20 @@ def tile_picked_forkcrossbsendgap_none_p_kernel(tc, x_words, x_scales, w1, gn, w
 
         nc.vector.tensor_copy(*deal_views(0, 0, 88))
         nc.scalar.copy(*deal_views(0, 88, P))
-        nc.vector.tensor_copy(xsg[:], xs[:].indirect(l_offs[:]))
+        nc.vector.tensor_copy(xsg_first[:], xs[:].indirect(part(l_offs, 0)))
         quantize(w_q[0], w_s[0], w_bf[0][:])
         for c in range(2):
             nc.vector.tensor_copy(xg[:, half(c)], xw[:].bitcast(U32).indirect(part(l_offs, c)))
+        xsg_second = sb.tile([P, HALF], U8, name="xsg_second", tag="xw", align_bytes=64)
+        nc.vector.tensor_copy(xsg_second[:], xs[:].indirect(part(l_offs, 1)))
+        xsg = (xsg_first, xsg_second)
 
         y_parts = [(0, half(0), banks[4][:, half(0)]), (0, half(1), banks[0][:, half(1)])]
         y_parts.extend((t, slice(0, S), banks[t][:]) for t in range(1, PACK))
-        for t, cols, acc in y_parts:
-            product(acc, 0, t, xg[:, cols], xsg[:, cols])
+        for c in range(2):
+            for t in range(PACK):
+                bank = banks[4] if (t, c) == (0, 0) else banks[t]
+                product(bank[:, half(c)], 0, t, xg[:, half(c)], xsg[c][:])
         for t, cols, acc in y_parts:
             nc.scalar.activation(ywin[t][:, S:][:, cols], acc, ACT.Relu)
         for t, cols, acc in y_parts:
@@ -146,11 +150,12 @@ def tile_picked_forkcrossbsendgap_none_p_kernel(tc, x_words, x_scales, w1, gn, w
         turned = [(banks[5], banks[6]), (banks[7], banks[4])]
         back = (banks[0], banks[1])
         for u in range(2):
-            for e in range(2):
-                t = 2 * u + e
-                for c in range(PACK):
-                    at = (c % 2) * HALF + e * P
-                    turn_add(turned[u][c // 2][:, at : at + P], ym[t][:, block(c)], dswin[t][:, block(c)])
+            for term, src in enumerate((ym, dswin)):
+                for e in range(2):
+                    for c in range(PACK):
+                        at = (c % 2) * HALF + e * P
+                        turn(turned[u][c // 2][:, at : at + P], src[2 * u + e][:, block(c)],
+                             start=(term, e, c % 2) == (0, 0, 0), stop=(term, e, c % 2) == (1, 1, 1))
             for h in range(2):
                 nc.scalar.copy(z_t[u][:, h * S : (h + 1) * S].rearrange("j (c p e) -> j c p e", c=2, e=2),
                                turned[u][h][:].rearrange("j (c e p) -> j c p e", c=2, e=2))
@@ -181,6 +186,9 @@ def tile_picked_forkcrossbsendgap_none_p_kernel(tc, x_words, x_scales, w1, gn, w
                 product(b_banks[t][:, half(c)], 2, t, z2_q[c][:], z2_s[c][:])
                 nc.scalar.copy(bwin[t][:, half(c)], b_banks[t][:, half(c)])
 
+        def a_plus(t, c):
+            nc.scalar.activation(apos[t][:, half(c)], a_banks[t][:, half(c)], ACT.Copy, scale=0.75)
+
         def q_gather(t, c):
             nc.vector.tensor_tensor(qt[t][:, half(c)], awin[t][:].indirect(part(l4, c)), bwin[t][:, half(c)], ALU.mult)
 
@@ -196,34 +204,53 @@ def tile_picked_forkcrossbsendgap_none_p_kernel(tc, x_words, x_scales, w1, gn, w
             nc.scalar.activation(awin[t][:], a_banks[t][:], ACT.Copy, scale=-0.75)
             if t == 0:
                 z2_interleave(0)
-        for t in range(2):
-            nc.scalar.activation(apos[t][:], a_banks[t][:], ACT.Copy, scale=0.75)
         z2_fetch(1)
         b_products(0)
+        for t in range(2):
+            a_plus(t, 0)
         z2_subtract(1, range(PACK))
         for t in range(2):
             q_gather(t, 0)
         z2_interleave(1)
-        b_products(1)
         for t in range(2, PACK):
-            nc.scalar.activation(apos[t][:], a_banks[t][:], ACT.Copy, scale=0.75)
+            a_plus(t, 0)
+        b_products(1)
+        for t in range(2):
+            a_plus(t, 1)
         for t in range(2, PACK):
             q_gather(t, 0)
         out_rows = out.rearrange("(p t) n -> p t n", t=PACK)
-        for t in range(PACK - 1):
+
+        def p_gather(t, c, factor):
+            nc.vector.tensor_tensor(pt[t][:, half(c)], bwin[t][:].indirect(part(l5, c)), factor[t][:, half(c)], ALU.mult)
+
+        def store(t, c):
+            nc.sync.dma_start(out_rows[:, t, half(c)], ot[t][:, half(c)])
+
+        def add_on_tensor(t, c, bank):
+            for term, src in enumerate((qt, pt)):
+                for k in range(2):
+                    turn(bank[:, block(k)], src[t][:, block(2 * c + k)], start=(term, k) == (0, 0), stop=(term, k) == (1, 1))
+            nc.scalar.copy(st[t][:, half(c)], bank[:, half(0)])
+            for k in range(2):
+                nc.tensor.transpose(bank[:, block(2 + k)], st[t][:, block(2 * c + k)], ident[:])
+            nc.scalar.copy(ot[t][:, half(c)], bank[:, half(1)])
+            store(t, c)
+
+        def subtract_on_vector(t, c):
+            nc.vector.tensor_tensor(ot[t][:, half(c)], qt[t][:, half(c)], pt[t][:, half(c)], ALU.subtract)
+            store(t, c)
+
+        for t in range(PACK):
+            p_gather(t, 0, apos)
+            add_on_tensor(t, 0, b_banks[t])
+        for t in range(2):
             q_gather(t, 1)
-            nc.vector.tensor_tensor(pt[t][:], bwin[t][:].indirect(l5[:]), apos[t][:], ALU.mult)
-            there, again = a_banks[2 * (t % 2)], a_banks[2 * (t % 2) + 1]
-            for c in range(PACK):
-                turn_add(there[:, block(c)], qt[t][:, block(c)], pt[t][:, block(c)])
-            nc.scalar.copy(st[t][:], there[:])
-            for c in range(PACK):
-                nc.tensor.transpose(again[:, block(c)], st[t][:, block(c)], ident[:])
-            nc.scalar.copy(ot[t][:], again[:])
-            nc.sync.dma_start(out_rows[:, t, :], ot[t][:])
+            p_gather(t, 1, apos)
+            add_on_tensor(t, 1, a_banks[t])
+        q_gather(2, 1)
+        p_gather(2, 1, awin)
         q_gather(3, 1)
-        for c in range(2):
-            nc.vector.tensor_tensor(pt[3][:, half(c)], bwin[3][:].indirect(part(l5, c)), apos[3][:, half(c)], ALU.mult)
-        for c in range(2):
-            nc.vector.tensor_tensor(ot[3][:, half(c)], pt[3][:, half(c)], qt[3][:, half(c)], ALU.add)
-            nc.sync.dma_start(out_rows[:, 3, half(c)], ot[3][:, half(c)])
+        subtract_on_vector(2, 1)
+        p_gather(3, 1, awin)
+        subtract_on_vector(3, 1)

@@ -50,18 +50,17 @@ def tile_picked_forkcrossbsendgap_none_p_kernel(tc, x_words, x_scales, w1, gn, w
         apos = tiles("apos", [P, S], F32)
         ym = tiles("ym", [P, S], F32)
         ident = sb.tile([P, P], F32, name="ident", align_bytes=64)
-        z_t = tiles("z_t", [P, 2 * S], BF16, 2)
-        zbuf = sb.tile([P, 3 * S], F32, name="zbuf", align_bytes=64)
-        z_words = zbuf[:, S:]
+        z_words = tiles("z_words", [P, S], F32, 2)
         z_q = sb.tile([P, S], U32, name="z_q", align_bytes=64)
         z_s = sb.tile([P, S], U8, name="z_s", align_bytes=64)
         g3_first = tiles("g3", [P, HALF], F32)
-        g3 = [[g[:] for g in g3_first], [zbuf[:, 2 * S : 2 * S + HALF], zbuf[:, 2 * S + HALF :], g3_first[2][:], g3_first[3][:]]]
-        z2buf = sb.tile([P, 2 * S], F32, name="z2buf", align_bytes=64)
-        z2_f = [zbuf[:, : 2 * S], z2buf[:]]
+        z2_f = tiles("z2_f", [P, PACK * HALF], F32, 2)
+        g3 = [[g[:] for g in g3_first], [z2_f[0][:, :HALF], z2_f[0][:, HALF:S], z_words[1][:, :HALF], z_words[1][:, HALF:]]]
+        z_t_first = sb.tile([P, 2 * S], BF16, name="z_t_first", align_bytes=64)
+        z_t = [z_t_first[:], z2_f[0][:, S:].bitcast(BF16)]
+        z2_b = tiles("z2_b", [P, PACK * HALF], BF16, 2)
         pt = tiles("pt", [P, S], F32)
         qt = tiles("qt", [P, S], F32)
-        z2_b = [z2buf[:, :S].bitcast(BF16), qt[2][:].bitcast(BF16)]
         z2_q = tiles("z2_q", [P, HALF], U32, 2)
         z2_s = tiles("z2_s", [P, HALF], U8, 2)
         st = tiles("st", [P, S], F32)
@@ -72,8 +71,8 @@ def tile_picked_forkcrossbsendgap_none_p_kernel(tc, x_words, x_scales, w1, gn, w
             nc.sync.dma_start(w_raw[i][:], w.rearrange("(p j) c -> p j c", j=PACK))
 
         nc.vector.memset(xs[:].bitcast(I32), 0)
-        nc.sync.dma_start(gn_sb[:], gn.rearrange("(p t) o -> p (t o)", t=PACK))
         load_w(0, w1)
+        nc.sync.dma_start(gn_sb[:], gn.rearrange("(p t) o -> p (t o)", t=PACK))
         for q in range(4):
             nc.sync.dma_start(xs[32 * q : 32 * q + 4, :].bitcast(I32), x_scales[0, 4 * q : 4 * q + 4, :].bitcast(I32))
         nc.sync.dma_start(l_offs[:], offs)
@@ -93,7 +92,7 @@ def tile_picked_forkcrossbsendgap_none_p_kernel(tc, x_words, x_scales, w1, gn, w
             return dst[:, m0:m1], src[:, m0:m1]
 
         def quantize(codes, scales, src):
-            nc.vector.quantize_mx(out=codes[:].bitcast(FP8X4), scales=scales[:], in_=src)
+            nc.vector.quantize_mx(out=codes.bitcast(FP8X4), scales=scales, in_=src)
 
         def product(dst, i, t, codes, scales):
             cols = slice(P * t, P * (t + 1))
@@ -113,24 +112,23 @@ def tile_picked_forkcrossbsendgap_none_p_kernel(tc, x_words, x_scales, w1, gn, w
             nc.tensor.matmul(dst, src, ident[:], start=start, stop=stop, is_transpose=True)
 
         make_identity(nc, ident[:])
-        for t in range(PACK):
-            nc.vector.tensor_copy(bwin[t][:, S:], gn_sb[:, t : t + 1].to_broadcast([P, S]))
-        nc.vector.tensor_scalar(gh_sb[:], gn_sb[:], -0.5, None, ALU.mult)
-
         nc.vector.tensor_copy(*deal_views(0, 0, 88))
         nc.scalar.copy(*deal_views(0, 88, P))
+        for t in range(PACK):
+            nc.scalar.copy(bwin[t][:, S:], gn_sb[:, t : t + 1].to_broadcast([P, S]))
+        nc.scalar.activation(gh_sb[:], gn_sb[:], ACT.Copy, scale=-0.5)
         nc.vector.tensor_copy(xsg_first[:], xs[:].indirect(part(l_offs, 0)))
-        quantize(w_q[0], w_s[0], w_bf[0][:])
+        quantize(w_q[0][:], w_s[0][:], w_bf[0][:])
         for c in range(2):
             nc.vector.tensor_copy(xg[:, half(c)], xw[:].bitcast(U32).indirect(part(l_offs, c)))
         xsg_second = sb.tile([P, HALF], U8, name="xsg_second", tag="xw", align_bytes=64)
         nc.vector.tensor_copy(xsg_second[:], xs[:].indirect(part(l_offs, 1)))
         xsg = (xsg_first, xsg_second)
 
-        y_parts = [(0, half(0), banks[4][:, half(0)]), (0, half(1), banks[0][:, half(1)])]
-        y_parts.extend((t, slice(0, S), banks[t][:]) for t in range(1, PACK))
-        for c in range(2):
-            for t in range(PACK):
+        y_parts = [(0, half(0), banks[4][:, half(0)]), (1, slice(0, S), banks[1][:]), (0, half(1), banks[0][:, half(1)])]
+        y_parts.extend((t, slice(0, S), banks[t][:]) for t in range(2, PACK))
+        for c, order in enumerate(((0, 1, 2, 3), (1, 0, 2, 3))):
+            for t in order:
                 bank = banks[4] if (t, c) == (0, 0) else banks[t]
                 product(bank[:, half(c)], 0, t, xg[:, half(c)], xsg[c][:])
         for t, cols, acc in y_parts:
@@ -142,10 +140,9 @@ def tile_picked_forkcrossbsendgap_none_p_kernel(tc, x_words, x_scales, w1, gn, w
         nc.scalar.copy(*deal_views(1, 0, P))
         nc.scalar.copy(*deal_views(2, 0, P))
 
-        for c in range(2):
-            nc.vector.tensor_tensor(dswin[0][:].indirect(part(l1, c)), ywin[0][:, S:][:, half(c)], bwin[0][:, S:][:, half(c)], ALU.mult)
-        for t in range(1, PACK):
-            nc.vector.tensor_tensor(dswin[t][:].indirect(l1[:]), ywin[t][:, S:], bwin[t][:, S:], ALU.mult)
+        for t, cols, acc in y_parts:
+            places = l1[:, cols.start // 16 : cols.stop // 16]
+            nc.vector.tensor_tensor(dswin[t][:].indirect(places), ywin[t][:, S:][:, cols], bwin[t][:, S:][:, cols], ALU.mult)
 
         turned = [(banks[5], banks[6]), (banks[7], banks[4])]
         back = (banks[0], banks[1])
@@ -161,30 +158,31 @@ def tile_picked_forkcrossbsendgap_none_p_kernel(tc, x_words, x_scales, w1, gn, w
                                turned[u][h][:].rearrange("j (c e p) -> j c p e", c=2, e=2))
                 for c in range(2 * h, 2 * h + 2):
                     at = u * HALF + (c % 2) * P
-                    nc.tensor.transpose(back[h][:, at : at + P], z_t[u][:].bitcast(F32)[:, block(c)], ident[:])
-        for h in range(2):
-            nc.scalar.copy(z_words[:, h * S : (h + 1) * S].rearrange("p (j u) -> p j u", u=2),
-                           back[h][:].rearrange("p (u j) -> p j u", u=2))
+                    nc.tensor.transpose(back[h][:, at : at + P], z_t[u].bitcast(F32)[:, block(c)], ident[:])
 
-        def z2_fetch(c):
-            for t in range(PACK):
+        def piece(tile, t):
+            return tile[:, t * HALF : (t + 1) * HALF]
+
+        def z2_fetch(c, ts):
+            for t in ts:
                 nc.vector.tensor_copy(g3[c][t], ywin[t][:].indirect(part(l3, c)))
 
         def z2_subtract(c, ts):
             for t in ts:
-                nc.vector.tensor_tensor(z2_f[c][:, t * HALF : (t + 1) * HALF], ywin[t][:].indirect(part(l2, c)), g3[c][t], ALU.subtract)
+                nc.vector.tensor_tensor(piece(z2_f[c], t), ywin[t][:].indirect(part(l2, c)), g3[c][t], ALU.subtract)
 
-        def z2_interleave(c):
-            nc.scalar.copy(z2_b[c].rearrange("p (c i t) -> p c t i", i=4, t=PACK), z2_f[c].rearrange("p (t c i) -> p c t i", t=PACK, i=4))
+        def z2_interleave(dst, src):
+            nc.scalar.copy(dst.rearrange("p (c i t) -> p c t i", i=4, t=PACK), src.rearrange("p t (c i) -> p c t i", i=4))
 
         a_banks = (banks[2], banks[3], banks[5], banks[6])
         b_banks = (banks[7], banks[4], banks[0], banks[1])
 
         def b_products(c):
-            quantize(z2_q[c], z2_s[c], z2_b[c])
             for t in range(PACK):
                 product(b_banks[t][:, half(c)], 2, t, z2_q[c][:], z2_s[c][:])
-                nc.scalar.copy(bwin[t][:, half(c)], b_banks[t][:, half(c)])
+
+        def b_out(t, c):
+            nc.scalar.copy(bwin[t][:, half(c)], b_banks[t][:, half(c)])
 
         def a_plus(t, c):
             nc.scalar.activation(apos[t][:, half(c)], a_banks[t][:, half(c)], ACT.Copy, scale=0.75)
@@ -192,33 +190,43 @@ def tile_picked_forkcrossbsendgap_none_p_kernel(tc, x_words, x_scales, w1, gn, w
         def q_gather(t, c):
             nc.vector.tensor_tensor(qt[t][:, half(c)], awin[t][:].indirect(part(l4, c)), bwin[t][:, half(c)], ALU.mult)
 
-        z2_fetch(0)
-        z2_subtract(0, range(2))
-        quantize(w_q[1], w_s[1], w_bf[1][:])
-        quantize(w_q[2], w_s[2], w_bf[2][:])
-        quantize(z_q, z_s, z_words.bitcast(BF16))
-        z2_subtract(0, range(2, PACK))
+        z2_fetch(0, range(PACK))
+        z2_subtract(0, (0, 1))
+        quantize(w_q[1][:], w_s[1][:], w_bf[1][:])
+        quantize(w_q[2][:], w_s[2][:], w_bf[2][:])
+        for h in range(2):
+            nc.scalar.copy(z_words[h][:].rearrange("p (j u) -> p j u", u=2), back[h][:].rearrange("p (u j) -> p j u", u=2))
+            quantize(z_q[:, half(h)], z_s[:, half(h)], z_words[h][:].bitcast(BF16))
+        z2_subtract(0, (2, 3))
         for t in range(PACK):
             product(a_banks[t][:], 1, t, z_q[:], z_s[:])
+        z2_rows = [z2_f[c][:].rearrange("p (t n) -> p t n", t=PACK) for c in range(2)]
+        z2_interleave(z2_b[0][:], z2_rows[0])
         for t in range(PACK):
             nc.scalar.activation(awin[t][:], a_banks[t][:], ACT.Copy, scale=-0.75)
-            if t == 0:
-                z2_interleave(0)
-        z2_fetch(1)
+        z2_fetch(1, (2, 3))
+        z2_subtract(1, (2, 3))
+        quantize(z2_q[0][:], z2_s[0][:], z2_b[0][:])
         b_products(0)
+        z2_fetch(1, (0, 1))
+        z2_subtract(1, (0, 1))
+        for t in range(2):
+            b_out(t, 0)
         for t in range(2):
             a_plus(t, 0)
-        z2_subtract(1, range(PACK))
-        for t in range(2):
             q_gather(t, 0)
-        z2_interleave(1)
+        z2_interleave(z2_b[1][:], z2_rows[1])
+        quantize(z2_q[1][:], z2_s[1][:], z2_b[1][:])
         for t in range(2, PACK):
-            a_plus(t, 0)
+            b_out(t, 0)
+            q_gather(t, 0)
         b_products(1)
+        a_plus(2, 0)
+        for t in range(PACK):
+            b_out(t, 1)
+        a_plus(3, 0)
         for t in range(2):
             a_plus(t, 1)
-        for t in range(2, PACK):
-            q_gather(t, 0)
         out_rows = out.rearrange("(p t) n -> p t n", t=PACK)
 
         def p_gather(t, c, factor):
@@ -251,6 +259,6 @@ def tile_picked_forkcrossbsendgap_none_p_kernel(tc, x_words, x_scales, w1, gn, w
         q_gather(2, 1)
         p_gather(2, 1, awin)
         q_gather(3, 1)
-        subtract_on_vector(2, 1)
         p_gather(3, 1, awin)
+        subtract_on_vector(2, 1)
         subtract_on_vector(3, 1)

from contextlib import ExitStack

import concourse.mybir as mybir
from concourse.masks import make_identity

F32 = mybir.dt.float32
BF16 = mybir.dt.bfloat16
I32 = mybir.dt.int32
U32 = mybir.dt.uint32
U16 = mybir.dt.uint16
U8 = mybir.dt.uint8
FP8X4 = mybir.dt.float8_e4m3fn_x4
ALU = mybir.AluOpType
ACT = mybir.ActivationFunctionType

P = 128
PACK = 4
T = 2048
S = 512
HALF = S // 2
FLOPS = 3 * 2 * 512 * 512 * 512


def tile_picked_forkcrossbsendgap_none_p_kernel(tc, x_words, x_scales, w1, gn, w2, gm, w3, offs, n1, n2, n3, n4, n5, out):
    nc = tc.nc
    with ExitStack() as ctx:
        sb = ctx.enter_context(tc.tile_pool(name="sb", bufs=1))
        ps = ctx.enter_context(tc.psum_pool(name="ps", bufs=1))

        def tiles(name, shape, dtype, count=PACK):
            return [sb.tile(shape, dtype, name="%s%d" % (name, i), align_bytes=64) for i in range(count)]

        lists = tiles("list", [P, S // 16], U16, 6)
        l_offs, l1, l2, l3, l4, l5 = lists
        xw = sb.tile([P, T], I32, name="xw", tag="xw", align_bytes=64)
        xs = sb.tile([P, T], U8, name="xs", align_bytes=64)
        gn_sb = sb.tile([P, PACK], F32, name="gn_sb", align_bytes=64)
        gm_sb = sb.tile([P, PACK], F32, name="gm_sb", align_bytes=64)
        gh_sb = sb.tile([P, PACK], F32, name="gh_sb", align_bytes=64)
        w_raw = tiles("w_raw", [P, PACK, S], F32, 3)
        w_bf = tiles("w_bf", [P, PACK * S], BF16, 3)
        w_q = tiles("w_q", [P, S], U32, 3)
        w_s = tiles("w_s", [P, S], U8, 3)
        xg = sb.tile([P, S], U32, name="xg", align_bytes=64)
        xsg_first = sb.tile([P, HALF], U8, name="xsg_first", align_bytes=64)
        ywin = tiles("ywin", [P, 2 * S], F32)
        dswin = tiles("dswin", [P, 2 * S], F32)
        bwin = tiles("bwin", [P, 2 * S], F32)
        awin = tiles("awin", [P, S], F32)
        apos = tiles("apos", [P, S], F32)
        ym = tiles("ym", [P, S], F32)
        ident = sb.tile([P, P], F32, name="ident", align_bytes=64)
        z_words = tiles("z_words", [P, S], F32, 2)
        z_q = sb.tile([P, S], U32, name="z_q", align_bytes=64)
        z_s = sb.tile([P, S], U8, name="z_s", align_bytes=64)
        g3_first = tiles("g3", [P, HALF], F32)
        z2_f = tiles("z2_f", [P, PACK * HALF], F32, 2)
        g3 = [[g[:] for g in g3_first], [z2_f[0][:, :HALF], z2_f[0][:, HALF:S], z_words[1][:, :HALF], z_words[1][:, HALF:]]]
        z_t_first = sb.tile([P, 2 * S], BF16, name="z_t_first", align_bytes=64)
        z_t = [z_t_first[:], z2_f[0][:, S:].bitcast(BF16)]
        z2_b = tiles("z2_b", [P, PACK * HALF], BF16, 2)
        pt = tiles("pt", [P, S], F32)
        qt = tiles("qt", [P, S], F32)
        z2_q = tiles("z2_q", [P, HALF], U32, 2)
        z2_s = tiles("z2_s", [P, HALF], U8, 2)
        st = tiles("st", [P, S], F32)
        ot = tiles("ot", [P, S], F32)
        banks = [ps.tile([P, S], F32, name="bank%d" % i) for i in range(8)]

        def load_w(i, w):
            nc.sync.dma_start(w_raw[i][:], w.rearrange("(p j) c -> p j c", j=PACK))

        nc.vector.memset(xs[:].bitcast(I32), 0)
        load_w(0, w1)
        nc.sync.dma_start(gn_sb[:], gn.rearrange("(p t) o -> p (t o)", t=PACK))
        for q in range(4):
            nc.sync.dma_start(xs[32 * q : 32 * q + 4, :].bitcast(I32), x_scales[0, 4 * q : 4 * q + 4, :].bitcast(I32))
        nc.sync.dma_start(l_offs[:], offs)
        nc.sync.dma_start(xw[:], x_words[0].rearrange("p n t -> p (n t)").bitcast(I32))
        nc.sync.dma_start(l1[:], n1)
        load_w(1, w2)
        nc.sync.dma_start(gm_sb[:], gm.rearrange("(p t) o -> p (t o)", t=PACK))
        nc.sync.dma_start(l2[:], n2)
        nc.sync.dma_start(l3[:], n3)
        load_w(2, w3)
        nc.sync.dma_start(l4[:], n4)
        nc.sync.dma_start(l5[:], n5)

        def deal_views(i, m0, m1):
            dst = w_bf[i][:].rearrange("p (t m j) -> p m j t", t=PACK, j=PACK)
            src = w_raw[i][:].rearrange("p j (m t) -> p m j t", t=PACK)
            return dst[:, m0:m1], src[:, m0:m1]

        def quantize(codes, scales, src):
            nc.vector.quantize_mx(out=codes.bitcast(FP8X4), scales=scales, in_=src)

        def product(dst, i, t, codes, scales):
            cols = slice(P * t, P * (t + 1))
            nc.tensor.matmul_mx(out=dst, lhsT=w_q[i][:, cols].bitcast(FP8X4), lhsT_scale=w_s[i][:, cols],
                                rhs=codes.bitcast(FP8X4), rhs_scale=scales, start=True, stop=True)

        def part(lst, c):
            return lst[:, c * HALF // 16 : (c + 1) * HALF // 16]

        def half(c):
            return slice(c * HALF, (c + 1) * HALF)

        def block(c):
            return slice(c * P, (c + 1) * P)

        def turn(dst, src, start, stop):
            nc.tensor.matmul(dst, src, ident[:], start=start, stop=stop, is_transpose=True)

        make_identity(nc, ident[:])
        nc.vector.tensor_copy(*deal_views(0, 0, 88))
        nc.scalar.copy(*deal_views(0, 88, P))
        for t in range(PACK):
            nc.scalar.copy(bwin[t][:, S:], gn_sb[:, t : t + 1].to_broadcast([P, S]))
        nc.scalar.activation(gh_sb[:], gn_sb[:], ACT.Copy, scale=-0.5)
        nc.vector.tensor_copy(xsg_first[:], xs[:].indirect(part(l_offs, 0)))
        quantize(w_q[0][:], w_s[0][:], w_bf[0][:])
        for c in range(2):
            nc.vector.tensor_copy(xg[:, half(c)], xw[:].bitcast(U32).indirect(part(l_offs, c)))
        xsg_second = sb.tile([P, HALF], U8, name="xsg_second", tag="xw", align_bytes=64)
        nc.vector.tensor_copy(xsg_second[:], xs[:].indirect(part(l_offs, 1)))
        xsg = (xsg_first, xsg_second)

        y_parts = [(0, half(0), banks[4][:, half(0)]), (1, slice(0, S), banks[1][:]), (0, half(1), banks[0][:, half(1)])]
        y_parts.extend((t, slice(0, S), banks[t][:]) for t in range(2, PACK))
        for c, order in enumerate(((0, 1, 2, 3), (1, 0, 2, 3))):
            for t in order:
                bank = banks[4] if (t, c) == (0, 0) else banks[t]
                product(bank[:, half(c)], 0, t, xg[:, half(c)], xsg[c][:])
        for t, cols, acc in y_parts:
            nc.scalar.activation(ywin[t][:, S:][:, cols], acc, ACT.Relu)
        for t, cols, acc in y_parts:
            nc.scalar.activation(ym[t][:, cols], acc, ACT.Copy, scale=gh_sb[:, t : t + 1])
        for t, cols, acc in y_parts:
            nc.scalar.activation(ywin[t][:, cols], acc, ACT.Copy, scale=gm_sb[:, t : t + 1])
        nc.scalar.copy(*deal_views(1, 0, P))
        nc.scalar.copy(*deal_views(2, 0, P))

        for t, cols, acc in y_parts:
            places = l1[:, cols.start // 16 : cols.stop // 16]
            nc.vector.tensor_tensor(dswin[t][:].indirect(places), ywin[t][:, S:][:, cols], bwin[t][:, S:][:, cols], ALU.mult)

        turned = [(banks[5], banks[6]), (banks[7], banks[4])]
        back = (banks[0], banks[1])
        for u in range(2):
            for term, src in enumerate((ym, dswin)):
                for e in range(2):
                    for c in range(PACK):
                        at = (c % 2) * HALF + e * P
                        turn(turned[u][c // 2][:, at : at + P], src[2 * u + e][:, block(c)],
                             start=(term, e, c % 2) == (0, 0, 0), stop=(term, e, c % 2) == (1, 1, 1))
            for h in range(2):
                nc.scalar.copy(z_t[u][:, h * S : (h + 1) * S].rearrange("j (c p e) -> j c p e", c=2, e=2),
                               turned[u][h][:].rearrange("j (c e p) -> j c p e", c=2, e=2))
                for c in range(2 * h, 2 * h + 2):
                    at = u * HALF + (c % 2) * P
                    nc.tensor.transpose(back[h][:, at : at + P], z_t[u].bitcast(F32)[:, block(c)], ident[:])

        def piece(tile, t):
            return tile[:, t * HALF : (t + 1) * HALF]

        def z2_fetch(c, ts):
            for t in ts:
                nc.vector.tensor_copy(g3[c][t], ywin[t][:].indirect(part(l3, c)))

        def z2_subtract(c, ts):
            for t in ts:
                nc.vector.tensor_tensor(piece(z2_f[c], t), ywin[t][:].indirect(part(l2, c)), g3[c][t], ALU.subtract)

        def z2_interleave(dst, src):
            nc.scalar.copy(dst.rearrange("p (c i t) -> p c t i", i=4, t=PACK), src.rearrange("p t (c i) -> p c t i", i=4))

        a_banks = (banks[2], banks[3], banks[5], banks[6])
        b_banks = (banks[7], banks[4], banks[0], banks[1])

        def b_products(c):
            for t in range(PACK):
                product(b_banks[t][:, half(c)], 2, t, z2_q[c][:], z2_s[c][:])

        def b_out(t, c):
            nc.scalar.copy(bwin[t][:, half(c)], b_banks[t][:, half(c)])

        def a_plus(t, c):
            nc.scalar.activation(apos[t][:, half(c)], a_banks[t][:, half(c)], ACT.Copy, scale=0.75)

        def q_gather(t, c):
            nc.vector.tensor_tensor(qt[t][:, half(c)], awin[t][:].indirect(part(l4, c)), bwin[t][:, half(c)], ALU.mult)

        z2_fetch(0, range(PACK))
        z2_subtract(0, (0, 1))
        quantize(w_q[1][:], w_s[1][:], w_bf[1][:])
        quantize(w_q[2][:], w_s[2][:], w_bf[2][:])
        for h in range(2):
            nc.scalar.copy(z_words[h][:].rearrange("p (j u) -> p j u", u=2), back[h][:].rearrange("p (u j) -> p j u", u=2))
            quantize(z_q[:, half(h)], z_s[:, half(h)], z_words[h][:].bitcast(BF16))
        z2_subtract(0, (2, 3))
        for t in range(PACK):
            product(a_banks[t][:], 1, t, z_q[:], z_s[:])
        z2_rows = [z2_f[c][:].rearrange("p (t n) -> p t n", t=PACK) for c in range(2)]
        z2_interleave(z2_b[0][:], z2_rows[0])
        for t in range(PACK):
            nc.scalar.activation(awin[t][:], a_banks[t][:], ACT.Copy, scale=-0.75)
        z2_fetch(1, (2, 3))
        z2_subtract(1, (2, 3))
        quantize(z2_q[0][:], z2_s[0][:], z2_b[0][:])
        b_products(0)
        z2_fetch(1, (0, 1))
        z2_subtract(1, (0, 1))
        for t in range(2):
            b_out(t, 0)
        for t in range(2):
            a_plus(t, 0)
            q_gather(t, 0)
        z2_interleave(z2_b[1][:], z2_rows[1])
        quantize(z2_q[1][:], z2_s[1][:], z2_b[1][:])
        for t in range(2, PACK):
            b_out(t, 0)
            q_gather(t, 0)
        b_products(1)
        a_plus(2, 0)
        for t in range(PACK):
            b_out(t, 1)
        a_plus(3, 0)
        for t in range(2):
            a_plus(t, 1)
        out_rows = out.rearrange("(p t) n -> p t n", t=PACK)

        def p_gather(t, c, factor):
            nc.vector.tensor_tensor(pt[t][:, half(c)], bwin[t][:].indirect(part(l5, c)), factor[t][:, half(c)], ALU.mult)

        def store(t, c):
            nc.sync.dma_start(out_rows[:, t, half(c)], ot[t][:, half(c)])

        def add_on_tensor(t, c, bank):
            for term, src in enumerate((qt, pt)):
                for k in range(2):
                    turn(bank[:, block(k)], src[t][:, block(2 * c + k)], start=(term, k) == (0, 0), stop=(term, k) == (1, 1))
            nc.scalar.copy(st[t][:, half(c)], bank[:, half(0)])
            for k in range(2):
                nc.tensor.transpose(bank[:, block(2 + k)], st[t][:, block(2 * c + k)], ident[:])
            nc.scalar.copy(ot[t][:, half(c)], bank[:, half(1)])
            store(t, c)

        def subtract_on_vector(t, c):
            nc.vector.tensor_tensor(ot[t][:, half(c)], qt[t][:, half(c)], pt[t][:, half(c)], ALU.subtract)
            store(t, c)

        for t in range(PACK):
            p_gather(t, 0, apos)
            add_on_tensor(t, 0, b_banks[t])
        for t in range(2):
            q_gather(t, 1)
            p_gather(t, 1, apos)
            add_on_tensor(t, 1, a_banks[t])
        q_gather(2, 1)
        p_gather(2, 1, awin)
        q_gather(3, 1)
        p_gather(3, 1, awin)
        subtract_on_vector(2, 1)
        subtract_on_vector(3, 1)
